import numpy as np
import ml_dtypes


def mxq(x, axis, fmt="e4m3"):
    dtype, down = {"e4m3": (ml_dtypes.float8_e4m3fn, 7), "e5m2": (ml_dtypes.float8_e5m2, 14)}[fmt]
    v = np.moveaxis(np.asarray(x, np.float32).astype(ml_dtypes.bfloat16).astype(np.float64), axis, -1)
    blocks = v.reshape(v.shape[:-1] + (-1, 32))
    amax = np.abs(blocks).max(-1, keepdims=True)
    byte = np.maximum(np.where(amax > 0, np.frexp(amax)[1] - 1 + 127, 0) - down, 1)
    scale = np.exp2(byte - 127.0)
    codes = (blocks / scale).astype(np.float32).astype(dtype).astype(np.float64)
    return np.moveaxis((codes * scale).reshape(v.shape), -1, axis)


WIDE = False


def mx_kscale(k):
    if not WIDE:
        return np.ones(k)
    levels = np.array([10, -10, 5, -5, 0])
    if k % 512:
        return np.exp2(np.random.permutation(np.resize(levels, k // 32))).repeat(32)
    a = np.empty((k // 512, 16))
    for p in range(k // 512):
        a[p, :8] = np.random.permutation(np.resize(levels, 8))
        for g in range(8):
            far = levels[np.abs(levels - a[p, g]) >= 10]
            a[p, g + 8] = far[np.random.randint(len(far))]
    return np.exp2(a.ravel()).repeat(32)


def f64(x):
    return np.asarray(x).astype(np.float64)


def striped(idx):
    return np.tile(idx.reshape(-1, 16).T, (8, 1)).astype(np.uint16)


def unstriped(offs):
    return offs[:16].T.reshape(-1).astype(np.int64)


E2M1 = np.array([0.0, 0.5, 1.0, 1.5, 2.0, 3.0, 4.0, 6.0, -0.0, -0.5, -1.0, -1.5, -2.0, -3.0, -4.0, -6.0])


def pack_weight(w, fmt):
    k, n = w.shape
    w = f64(np.asarray(w, np.float32).astype(ml_dtypes.bfloat16)).reshape(k // 32, 32, n)
    amax = np.abs(w).max(1)
    if fmt == "e4m3":
        byte = np.frexp(amax)[1] - 1 + 127 - 7
    else:
        mant, ex = np.frexp(amax / 6.0)
        byte = np.where(mant > 0.5, ex, ex - 1) + 127
    byte = np.clip(np.where(amax > 0, byte, 1), 1, 254)
    scaled = (w * np.exp2(127.0 - byte)[:, None, :]).reshape(k, n).astype(np.float32)
    by_word = np.ascontiguousarray(scaled.reshape(k // 512, 128, 4, n).transpose(0, 1, 3, 2))
    if fmt == "e4m3":
        words = by_word.astype(ml_dtypes.float8_e4m3fn).view(np.uint8)
    else:
        c = by_word.astype(ml_dtypes.float4_e2m1fn).view(np.uint8) & 0xF
        words = (c[..., 0::2] | (c[..., 1::2] << 4)).reshape(k // 512, 128, 2 * n)
    return np.ascontiguousarray(words), np.ascontiguousarray(byte.astype(np.uint8).reshape(k // 512, 16, n))


def unpack_weight(words, scales, fmt):
    g, _, n = scales.shape
    words = np.ascontiguousarray(words).reshape(g, 128, n, -1)
    if fmt == "e4m3":
        vals = words.view(ml_dtypes.float8_e4m3fn).astype(np.float64)
    else:
        nib = np.empty((g, 128, n, 4), np.uint8)
        nib[..., 0::2] = words & 0xF
        nib[..., 1::2] = words >> 4
        vals = E2M1[nib]
    vals = vals * np.repeat(np.exp2(scales.astype(np.float64) - 127.0), 8, axis=1)[..., None]
    return vals.transpose(0, 1, 3, 2).reshape(g * 512, n)


def gelu(v):
    return 0.5 * v * (1.0 + np.tanh(np.sqrt(2.0 / np.pi) * (v + 0.044715 * v**3)))


K, T, E, C, H, N = 1024, 512, 4, 256, 512, 384


def by_expert(wq, xq):
    return np.concatenate([wq[e].T @ xq[:, e * C:(e + 1) * C] for e in range(E)], axis=1)


def setup_inputs():
    n = np.random.standard_normal
    s = mx_kscale(K)[:, None]
    u = mx_kscale(H)
    first = np.random.permutation(np.repeat(np.arange(E), T // E))
    second = (first + 1 + np.random.permutation(np.repeat(np.arange(E - 1), -(-T // (E - 1)))[:T])) % E
    while np.bincount(second, minlength=E).max() != T // E:
        load = np.bincount(second, minlength=E); hi, lo = int(load.argmax()), int(load.argmin())
        t = np.flatnonzero((second == hi) & (first != lo))[0]; second[t] = lo
    slot_token = np.empty(E * C, np.int64); pos = np.empty((2, T), np.int64); fill = np.zeros(E, np.int64)
    place = np.stack([np.random.permutation(C) for _ in range(E)])
    for r, deal in enumerate((first, second)):
        for t in np.random.permutation(T):
            e = deal[t]; j = e * C + place[e, fill[e]]; fill[e] += 1; slot_token[j] = t; pos[r, t] = j
    g = np.random.uniform(0.2, 0.8, T)
    w1 = [pack_weight(m, "e2m1") for m in n((E, K, H)) / np.sqrt(K) / s[None]]
    w3 = [pack_weight(m, "e2m1") for m in n((E, K, H)) / np.sqrt(K) / s[None] * u[None, None, :]]
    w2 = [pack_weight(m, "e2m1") for m in n((E, H, N)) / np.sqrt(H) / u[None, :, None]]
    return {
        "xT": (n((K, T)) * s).astype(np.float32),
        "w1_words": np.stack([m[0] for m in w1]),
        "w1_scales": np.stack([m[1] for m in w1]),
        "w3_words": np.stack([m[0] for m in w3]),
        "w3_scales": np.stack([m[1] for m in w3]),
        "w2_words": np.stack([m[0] for m in w2]),
        "w2_scales": np.stack([m[1] for m in w2]),
        "gate": np.stack([np.tile(g, (N, 1)), np.tile(1.0 - g, (N, 1))]).astype(np.float32),
        "offs": striped(slot_token),
        "pos1": striped(pos[0]),
        "pos2": striped(pos[1]),
    }


def reference(xT, w1_words, w1_scales, w3_words, w3_scales, w2_words, w2_scales, gate, offs, pos1, pos2):
    idx = unstriped(offs)
    w1 = np.stack([unpack_weight(w1_words[e], w1_scales[e], "e2m1") for e in range(E)])
    w3 = np.stack([unpack_weight(w3_words[e], w3_scales[e], "e2m1") for e in range(E)])
    w2 = np.stack([unpack_weight(w2_words[e], w2_scales[e], "e2m1") for e in range(E)])
    xq = mxq(f64(xT)[:, idx], 0, "e4m3")
    h = gelu(by_expert(w1, xq))
    h = h * by_expert(w3, xq)
    y = by_expert(w2, mxq(h, 0, "e4m3"))
    return f64(gate[0]) * y[:, unstriped(pos1)] + f64(gate[1]) * y[:, unstriped(pos2)]

from contextlib import ExitStack

import concourse.mybir as mybir
from concourse.masks import make_identity

K, T, E, C, H, N = 1024, 512, 4, 256, 512, 384
FLOPS = 2 * E * C * (2 * K * H + H * N)

F32 = mybir.dt.float32
BF16 = mybir.dt.bfloat16
I32 = mybir.dt.int32
U32 = mybir.dt.uint32
U16 = mybir.dt.uint16
U8 = mybir.dt.uint8
E4M3 = mybir.dt.float8_e4m3fn_x4
E2M1 = mybir.dt.float4_e2m1fn_x4
MULT = mybir.AluOpType.mult
ADD = mybir.AluOpType.add
GELU = mybir.ActivationFunctionType.Gelu_apprx_tanh

P = 128
PASSES = K // 512
NT = N // P
V_COLS = (176, 96)


def tile_moe_pln_glu_gelu_kernel(
    tc, xT, w1_words, w1_scales, w3_words, w3_scales, w2_words, w2_scales, gate, offs, pos1, pos2, out
):
    nc = tc.nc
    with ExitStack() as ctx:
        keep = ctx.enter_context(tc.tile_pool(name="keep", bufs=1))
        ring = ctx.enter_context(tc.tile_pool(name="ring", bufs=2))
        psum = ctx.enter_context(tc.psum_pool(name="psum", bufs=2))

        offs_t = keep.tile([P, 2 * T // 16], U16, name="offs_t")
        pos1_t = keep.tile([P, T // 16], U16, name="pos1_t")
        pos2_t = keep.tile([P, T // 16], U16, name="pos2_t")
        raw = [keep.tile([P, 4, T], F32, name=f"raw{s}") for s in range(PASSES)]
        grouped = [keep.tile([P, T, 4], BF16, name=f"grouped{s}", align_bytes=64) for s in range(PASSES)]
        xq = [keep.tile([P, T], U32, name=f"xq{s}", align_bytes=64) for s in range(PASSES)]
        xs = [keep.tile([P, T], U8, name=f"xs{s}", align_bytes=64) for s in range(PASSES)]
        gq = [[keep.tile([P, C], U32, name=f"gq{e}_{s}", align_bytes=64) for s in range(PASSES)] for e in range(E)]
        gs = [[keep.tile([P, C], U8, name=f"gs{e}_{s}", align_bytes=64) for s in range(PASSES)] for e in range(E)]
        w1t = keep.tile([P, E * PASSES, 2 * H], U8, name="w1t", align_bytes=64)
        w3t = keep.tile([P, E * PASSES, 2 * H], U8, name="w3t", align_bytes=64)
        w2t = keep.tile([P, E, 2 * N], U8, name="w2t", align_bytes=64)
        w1p = keep.tile([P, E * PASSES, H], U8, name="w1p", align_bytes=64)
        w3p = keep.tile([P, E * PASSES, H], U8, name="w3p", align_bytes=64)
        w2p = keep.tile([P, E, N], U8, name="w2p", align_bytes=64)
        gates = keep.tile([P, 2 * NT, T], F32, name="gates")
        ident = keep.tile([P, P], F32, name="ident")
        warm = keep.tile([P, 1], F32, name="warm")
        ys = [keep.tile([P, E * C], F32, name=f"ys{j}") for j in range(NT)]

        nc.vector.memset(w3p[:].rearrange("p a b -> p (a b)").bitcast(I32), 0)
        nc.vector.memset(w1p[:].rearrange("p a b -> p (a b)").bitcast(I32), 0)
        nc.vector.memset(warm[:], 0.0)
        nc.scalar.activation(warm[:], warm[:], GELU)
        nc.vector.memset(w2p[:].rearrange("p a b -> p (a b)").bitcast(I32), 0)
        nc.gpsimd.memset(xs[0][:], 0)
        nc.gpsimd.memset(xs[1][:], 0)

        def load_x(s, h):
            cols = slice(h * C, (h + 1) * C)
            nc.sync.dma_start(raw[s][:, :, cols], xT[s * 512 : (s + 1) * 512, cols].rearrange("(p j) w -> p j w", j=4))

        def load_words(e):
            for t, w in ((w1t, w1_words), (w3t, w3_words)):
                nc.sync.dma_start(
                    t[:, e * PASSES : (e + 1) * PASSES, :].bitcast(I32), w[e].rearrange("s p c -> p s c").bitcast(I32)
                )

        def load_scales(engine, t, w):
            rows = w.rearrange("e s q i -> q (e s) i")
            for q in range(4):
                engine.dma_start(t[32 * q : 32 * q + 4, :, :].bitcast(I32), rows[4 * q : 4 * q + 4].bitcast(I32))

        load_scales(nc.gpsimd, w3p, w3_scales)
        make_identity(nc, ident[:])
        load_x(0, 0)
        nc.sync.dma_start(offs_t[:], offs)
        load_x(0, 1)
        load_x(1, 0)
        load_x(1, 1)
        load_words(0)
        load_scales(nc.sync, w1p, w1_scales)
        load_words(1)
        load_scales(nc.sync, w2p, w2_scales)
        nc.sync.dma_start(w2t[:].bitcast(I32), w2_words.rearrange("e s p c -> p (e s) c").bitcast(I32))
        load_words(2)
        load_words(3)
        nc.sync.dma_start(pos1_t[:], pos1)
        nc.sync.dma_start(pos2_t[:], pos2)
        for g in range(2):
            nc.sync.dma_start(gates[:, g * NT : (g + 1) * NT, :], gate[g].rearrange("(j p) t -> p j t", p=P))

        def interleave(s, h):
            mid = h * C + V_COLS[s]
            for copy, a, b in ((nc.vector.tensor_copy, h * C, mid), (nc.scalar.copy, mid, (h + 1) * C)):
                copy(grouped[s][:, a:b, :], raw[s][:, :, a:b].rearrange("p j w -> p w j"))

        def quantize_x(s, h):
            cols = slice(h * C, (h + 1) * C)
            nc.vector.quantize_mx(
                out=xq[s][:, cols].bitcast(E4M3),
                scales=xs[s][:, cols],
                in_=grouped[s][:, cols, :].rearrange("p w j -> p (w j)"),
            )

        def gather(e, s):
            lists = offs_t[:, e * (C // 16) : (e + 1) * (C // 16)]
            nc.vector.tensor_copy(gq[e][s][:], xq[s][:].indirect(lists))
            nc.vector.tensor_copy(gs[e][s][:], xs[s][:].indirect(lists))

        acc = {}
        hid = {}
        turned = {}

        def up(e, h, passes):
            if 0 in passes:
                acc[e, h] = (psum.tile([P, H], F32, name="acc_a"), psum.tile([P, H], F32, name="acc_b"))
            slots = slice(h * P, (h + 1) * P)
            for bank, words, planes in zip(acc[e, h], (w1t, w3t), (w1p, w3p)):
                for s in passes:
                    nc.tensor.matmul_mx(
                        out=bank[:],
                        lhsT=gq[e][s][:, slots].bitcast(E4M3),
                        lhsT_scale=gs[e][s][:, slots],
                        rhs=words[:, e * PASSES + s, :].bitcast(E2M1),
                        rhs_scale=planes[:, e * PASSES + s, :],
                        start=(s == 0),
                        stop=(s == PASSES - 1),
                    )

        def pairs(bank):
            return bank[:].rearrange("p (m u d) -> p u m d", u=2, d=2)

        def glu(e, h):
            bank_a, bank_b = acc[e, h]
            act = ring.tile([P, H], F32, name="act")
            nc.scalar.activation(act[:].rearrange("p (u m d) -> p u m d", u=2, d=2), pairs(bank_a), GELU)
            prod = ring.tile([P, H], BF16, name="prod")
            flat = "p (u m d) -> p u m d"
            nc.vector.tensor_tensor(
                prod[:].rearrange(flat, u=2, d=2), act[:].rearrange(flat, u=2, d=2), pairs(bank_b), MULT
            )
            hid[e, h] = prod

        def turn(e, halves):
            bank = psum.tile([P, 2, 2, P], F32, name="bank_t")
            hg = ring.tile([P, C, 4], BF16, name="hg", align_bytes=64)
            dst = hg[:].rearrange("p r t -> p (r t)").bitcast(F32).rearrange("p (h r u) -> p h r u", h=2, u=2)
            for h in halves:
                words = hid[e, h][:].bitcast(F32)
                for u in range(2):
                    nc.tensor.transpose(bank[:, h, u, :], words[:, u * P : (u + 1) * P], ident[:])
            for h in halves:
                nc.scalar.copy(dst[:, h], bank[:, h].rearrange("p u r -> p r u"))
                turned[e, h] = hg

        def down(e, halves):
            first, width = halves[0] * P, len(halves) * P
            hq = ring.tile([P, C], U32, name="hq", align_bytes=64)
            hs = ring.tile([P, C], U8, name="hs", align_bytes=64)
            nc.vector.quantize_mx(
                out=hq[:, :width].bitcast(E4M3),
                scales=hs[:, :width],
                in_=turned[e, halves[0]][:, first : first + width, :].rearrange("p r t -> p (r t)"),
            )
            if width == C:
                bank01 = psum.tile([P, 2 * C], F32, name="bank_y")
                bank2 = psum.tile([P, 2 * C], F32, name="bank_y")
                parts = (bank01[:, :C], bank01[:, C:], bank2[:, :C])
            else:
                bank = psum.tile([P, 2 * C], F32, name="bank_y")
                parts = [bank[:, j * P : (j + 1) * P] for j in range(NT)]
            for j, y in enumerate(parts):
                nc.tensor.matmul_mx(
                    out=y,
                    lhsT=w2t[:, e, 2 * P * j : 2 * P * (j + 1)].bitcast(E2M1),
                    lhsT_scale=w2p[:, e, P * j : P * (j + 1)],
                    rhs=hq[:, :width].bitcast(E4M3),
                    rhs_scale=hs[:, :width],
                    start=True,
                    stop=True,
                )
            for j, y in enumerate(parts):
                nc.scalar.copy(ys[j][:, e * C + first : e * C + first + width], y)

        for h in range(2):
            interleave(0, h)
        for h in range(2):
            quantize_x(0, h)
        for h in range(2):
            interleave(1, h)
        for h in range(2):
            quantize_x(1, h)
        both = (0, 1)
        for s in range(PASSES):
            gather(0, s)
        up(0, 0, both)
        up(0, 1, both)
        glu(0, 0)
        for s in range(PASSES):
            gather(1, s)
        glu(0, 1)
        for e in range(1, E):
            up(e, 0, both)
            turn(e - 1, both)
            up(e, 1, both)
            glu(e, 0)
            if e == E - 1:
                turn(e, (0,))
            down(e - 1, both)
            glu(e, 1)
            if e + 1 < E:
                for s in range(PASSES):
                    gather(e + 1, s)
        down(E - 1, (0,))
        turn(E - 1, (1,))
        down(E - 1, (1,))

        for j in range(NT):
            first = ring.tile([P, T], F32, name="first")
            second = ring.tile([P, T], F32, name="second")
            total = ring.tile([P, T], F32, name="total")
            pieces = 2 if j == NT - 1 else 1
            for i in range(pieces):
                cols = slice(i * T // pieces, (i + 1) * T // pieces)
                listed = slice(cols.start // 16, cols.stop // 16)
                nc.vector.tensor_tensor(first[:, cols], ys[j][:].indirect(pos1_t[:, listed]), gates[:, j, cols], MULT)
                nc.vector.tensor_tensor(second[:, cols], ys[j][:].indirect(pos2_t[:, listed]), gates[:, NT + j, cols], MULT)
                nc.vector.tensor_tensor(total[:, cols], first[:, cols], second[:, cols], ADD)
                nc.sync.dma_start(out[j * P : (j + 1) * P, cols], total[:, cols])
